import numpy as np
import ml_dtypes


def mxq(x, axis, fmt="e4m3"):
    dtype, down = {"e4m3": (ml_dtypes.float8_e4m3fn, 7), "e5m2": (ml_dtypes.float8_e5m2, 14)}[fmt]
    v = np.moveaxis(np.asarray(x, np.float32).astype(ml_dtypes.bfloat16).astype(np.float64), axis, -1)
    blocks = v.reshape(v.shape[:-1] + (-1, 32))
    amax = np.abs(blocks).max(-1, keepdims=True)
    byte = np.maximum(np.where(amax > 0, np.frexp(amax)[1] - 1 + 127, 0) - down, 1)
    scale = np.exp2(byte - 127.0)
    codes = (blocks / scale).astype(np.float32).astype(dtype).astype(np.float64)
    return np.moveaxis((codes * scale).reshape(v.shape), -1, axis)


WIDE = False


def mx_kscale(k):
    if not WIDE:
        return np.ones(k)
    levels = np.array([30, -30])
    if k % 512:
        return np.exp2(np.random.permutation(np.resize(levels, k // 32))).repeat(32)
    a = np.empty((k // 512, 16))
    for p in range(k // 512):
        a[p, :8] = np.random.permutation(np.resize(levels, 8))
        for g in range(8):
            far = levels[np.abs(levels - a[p, g]) >= 10]
            a[p, g + 8] = far[np.random.randint(len(far))]
    return np.exp2(a.ravel()).repeat(32)


def f64(x):
    return np.asarray(x).astype(np.float64)


def striped(idx):
    return np.tile(np.asarray(idx).reshape(-1, 16).T, (8, 1)).astype(np.uint16)


def unstriped(offs):
    return offs[:16].T.reshape(-1).astype(np.int64)


E2M1 = np.array([0.0, 0.5, 1.0, 1.5, 2.0, 3.0, 4.0, 6.0, -0.0, -0.5, -1.0, -1.5, -2.0, -3.0, -4.0, -6.0])


def pack_weight(w, fmt):
    k, n = w.shape
    w = f64(np.asarray(w, np.float32).astype(ml_dtypes.bfloat16)).reshape(k // 32, 32, n)
    amax = np.abs(w).max(1)
    if fmt == "e4m3":
        byte = np.frexp(amax)[1] - 1 + 127 - 7
    else:
        mant, ex = np.frexp(amax / 6.0)
        byte = np.where(mant > 0.5, ex, ex - 1) + 127
    byte = np.clip(np.where(amax > 0, byte, 1), 1, 254)
    scaled = (w * np.exp2(127.0 - byte)[:, None, :]).reshape(k, n).astype(np.float32)
    by_word = np.ascontiguousarray(scaled.reshape(k // 512, 128, 4, n).transpose(0, 1, 3, 2))
    if fmt == "e4m3":
        words = by_word.astype(ml_dtypes.float8_e4m3fn).view(np.uint8)
    else:
        c = by_word.astype(ml_dtypes.float4_e2m1fn).view(np.uint8) & 0xF
        words = (c[..., 0::2] | (c[..., 1::2] << 4)).reshape(k // 512, 128, 2 * n)
    return np.ascontiguousarray(words), np.ascontiguousarray(byte.astype(np.uint8).reshape(k // 512, 16, n))


def unpack_weight(words, scales, fmt):
    g, _, n = scales.shape
    words = np.ascontiguousarray(words).reshape(g, 128, n, -1)
    if fmt == "e4m3":
        vals = words.view(ml_dtypes.float8_e4m3fn).astype(np.float64)
    else:
        nib = np.empty((g, 128, n, 4), np.uint8)
        nib[..., 0::2] = words & 0xF
        nib[..., 1::2] = words >> 4
        vals = E2M1[nib]
    vals = vals * np.repeat(np.exp2(scales.astype(np.float64) - 127.0), 8, axis=1)[..., None]
    return vals.transpose(0, 1, 3, 2).reshape(g * 512, n)


K, F, T, Z, J, R, N = 512, 512, 1024, 1024, 256, 512, 256


def setup_inputs():
    n = np.random.standard_normal
    idx = np.random.permutation(T)[:J]
    idx2 = np.random.permutation(Z)[:J]
    idx3 = np.random.permutation(J)[:J]
    idx4 = np.random.permutation(T)[:J]
    fk = mx_kscale(K)
    fr = mx_kscale(R)
    ff = mx_kscale(F)
    xtp = pack_weight(n((K, T)) / fk[:, None], "e2m1")
    wp = pack_weight(n((K, R)) * 1 / np.sqrt(K) * fk[:, None] * fr, "e4m3")
    xop = pack_weight(n((F, Z)) / ff[:, None], "e4m3")
    w2p = pack_weight(n((F, R)) * 1 / np.sqrt(F) * ff[:, None] * fr, "e2m1")
    wbp = pack_weight(n((R, N)) * 1 / np.sqrt(R) / fr[:, None], "e2m1")
    wsp = pack_weight(n((K, N)) * 1 / np.sqrt(K) * fk[:, None], "e4m3")
    return {
        "xt_words": xtp[0],
        "xt_scales": xtp[1],
        "w_words": wp[0],
        "w_scales": wp[1],
        "xo_words": xop[0],
        "xo_scales": xop[1],
        "w2_words": w2p[0],
        "w2_scales": w2p[1],
        "wb_words": wbp[0],
        "wb_scales": wbp[1],
        "ws_words": wsp[0],
        "ws_scales": wsp[1],
        "offs": striped(idx),
        "offs2": striped(idx2),
        "offs3": striped(idx3),
        "offs4": striped(idx4),
    }


def reference(xt_words, xt_scales, w_words, w_scales, xo_words, xo_scales, w2_words, w2_scales, wb_words, wb_scales, ws_words, ws_scales, offs, offs2, offs3, offs4):
    idx = unstriped(offs)
    idx2 = unstriped(offs2)
    idx3 = unstriped(offs3)
    idx4 = unstriped(offs4)
    xtu = unpack_weight(xt_words, xt_scales, "e2m1")
    wu = unpack_weight(w_words, w_scales, "e4m3")
    xou = unpack_weight(xo_words, xo_scales, "e4m3")
    w2u = unpack_weight(w2_words, w2_scales, "e2m1")
    wbu = unpack_weight(wb_words, wb_scales, "e2m1")
    wsu = unpack_weight(ws_words, ws_scales, "e4m3")
    xtidxg = xtu[:, idx]
    a = wu.T @ xtidxg
    xoidx2g = xou[:, idx2]
    b = w2u.T @ xoidx2g
    hid = np.maximum(a, b[:, idx3])
    hidq = mxq(hid, 0, "e5m2")
    xtidx4g = xtu[:, idx4]
    y = wbu.T @ hidq + wsu.T @ xtidx4g
    return y

@@ -1,0 +1,180 @@
+from contextlib import ExitStack
+
+import concourse.mybir as mybir
+
+F32 = mybir.dt.float32
+BF16 = mybir.dt.bfloat16
+I32 = mybir.dt.int32
+U32 = mybir.dt.uint32
+U16 = mybir.dt.uint16
+U8 = mybir.dt.uint8
+E4M3 = mybir.dt.float8_e4m3fn_x4
+E5M2 = mybir.dt.float8_e5m2_x4
+E2M1 = mybir.dt.float4_e2m1fn_x4
+COPY = mybir.ActivationFunctionType.Copy
+MAX = mybir.AluOpType.max
+
+P = 128
+PACK = 4
+T, Z, J, R, N = 1024, 1024, 256, 512, 256
+HALF = J // 2
+FLOPS = 2 * 512 * J * (R + R + N + N)
+
+
+def tile_list_partner_twotab_further_plain_kernel(
+    tc, xt_words, xt_scales, w_words, w_scales, xo_words, xo_scales, w2_words, w2_scales,
+    wb_words, wb_scales, ws_words, ws_scales, offs, offs2, offs3, offs4, out,
+):
+    nc = tc.nc
+    with ExitStack() as ctx:
+        sb = ctx.enter_context(tc.tile_pool(name="sb", bufs=1))
+        ps = ctx.enter_context(tc.psum_pool(name="ps", bufs=1))
+
+        def tile(name, shape, dtype):
+            return sb.tile(shape, dtype, name=name, align_bytes=64)
+
+        def load_list(name, src):
+            dst = tile(name, [P, J // 16], U16)
+            nc.sync.dma_start(dst[:], src)
+            return dst
+
+        def load_words(queue, name, src, cols, dtype):
+            dst = tile(name, [P, cols], dtype)
+            queue.dma_start(dst[:].bitcast(I32), src.bitcast(I32))
+            return dst
+
+        def load_scale_rows(queue, dst, src, q):
+            rows = src[0, 4 * q:4 * q + 4, :].bitcast(I32)
+            queue.dma_start(dst[32 * q:32 * q + 32, :].bitcast(I32), rows.unsqueeze(0).to_broadcast([8, *rows.shape]))
+
+        def fp8(words):
+            return words[0].rearrange("p c t -> p (c t)")
+
+        sy, sc, gp = nc.sync, nc.scalar, nc.gpsimd
+        xo_s = tile("xo_s", [P, Z], U8)
+        w2_s = tile("w2_s", [P, R], U8)
+        xt_s = tile("xt_s", [P, T], U8)
+        w_s = tile("w_s", [P, R], U8)
+        ws_s = tile("ws_s", [P, N], U8)
+        wb_s = tile("wb_s", [P, N], U8)
+        l2 = load_list("l2", offs2)
+        load_scale_rows(sc, xo_s, xo_scales, 0)
+        load_scale_rows(sy, xo_s, xo_scales, 1)
+        load_scale_rows(sc, xo_s, xo_scales, 2)
+        load_scale_rows(sy, xo_s, xo_scales, 3)
+        load_scale_rows(sc, w2_s, w2_scales, 0)
+        xo_w = load_words(sy, "xo_w", fp8(xo_words), Z, U32)
+        load_scale_rows(sc, w2_s, w2_scales, 1)
+        w2_w = load_words(gp, "w2_w", w2_words[0], R, U16)
+        load_scale_rows(gp, w2_s, w2_scales, 2)
+        load_scale_rows(sy, w2_s, w2_scales, 3)
+        w_w = load_words(sy, "w_w", fp8(w_words), R, U32)
+        l1 = load_list("l1", offs)
+        xt_w = load_words(sy, "xt_w", xt_words[0], T, U16)
+        load_scale_rows(sy, xt_s, xt_scales, 0)
+        load_scale_rows(sy, xt_s, xt_scales, 1)
+        load_scale_rows(sy, xt_s, xt_scales, 2)
+        load_scale_rows(sy, xt_s, xt_scales, 3)
+        l3 = load_list("l3", offs3)
+        load_scale_rows(sy, w_s, w_scales, 0)
+        load_scale_rows(sy, w_s, w_scales, 1)
+        load_scale_rows(sy, w_s, w_scales, 2)
+        load_scale_rows(sy, w_s, w_scales, 3)
+        l4 = load_list("l4", offs4)
+        ws_w = load_words(gp, "ws_w", fp8(ws_words), N, U32)
+        wb_w = load_words(gp, "wb_w", wb_words[0], N, U16)
+        load_scale_rows(sy, ws_s, ws_scales, 0)
+        load_scale_rows(sy, ws_s, ws_scales, 1)
+        load_scale_rows(sy, ws_s, ws_scales, 2)
+        load_scale_rows(sy, ws_s, ws_scales, 3)
+        load_scale_rows(gp, wb_s, wb_scales, 0)
+        load_scale_rows(gp, wb_s, wb_scales, 1)
+        load_scale_rows(sy, wb_s, wb_scales, 2)
+        load_scale_rows(sy, wb_s, wb_scales, 3)
+
+        def gather(name, window, offsets, dtype):
+            dst = tile(name, [P, J], dtype)
+            nc.vector.tensor_copy(dst[:], window[:].indirect(offsets[:]))
+            return dst
+
+        def deal(copy, name, src, dtype):
+            dst = tile(name, [P, PACK, P], dtype)
+            copy(dst[:].rearrange("p t m -> p m t"), src[:].rearrange("p (m t) -> p m t", t=PACK))
+            return dst
+
+        w2_wd = deal(nc.scalar.copy, "w2_wd", w2_w, U16)
+        w_wd = deal(nc.scalar.copy, "w_wd", w_w, U32)
+        xo_sg = gather("xo_sg", xo_s, l2, U8)
+        xo_wg = gather("xo_wg", xo_w, l2, U32)
+        w2_sd = deal(nc.vector.tensor_copy, "w2_sd", w2_s, U8)
+
+        b_sb = tile("b_sb", [P, PACK * J], F32)
+        for u in range(2):
+            bank = ps.tile([P, 2 * J], F32, name=f"b_bank{u}")
+            for e in range(2):
+                t = 2 * u + e
+                nc.tensor.matmul_mx(
+                    bank[:, e * J:(e + 1) * J],
+                    lhsT=w2_wd[:, t, :].bitcast(E2M1), lhsT_scale=w2_sd[:, t, :],
+                    rhs=xo_wg[:].bitcast(E4M3), rhs_scale=xo_sg[:], start=True, stop=True)
+            nc.scalar.copy(b_sb[:, 2 * u * J:2 * (u + 1) * J], bank[:])
+
+        xt_wg = gather("xt_wg", xt_w, l1, U16)
+        xt_sg = gather("xt_sg", xt_s, l1, U8)
+        w_sd = deal(nc.vector.tensor_copy, "w_sd", w_s, U8)
+
+        a_banks = []
+        for h in range(2):
+            cols = slice(h * HALF, (h + 1) * HALF)
+            bank = ps.tile([P, PACK, HALF], F32, name=f"a_bank{h}")
+            for t in range(PACK):
+                nc.tensor.matmul_mx(
+                    bank[:, t, :],
+                    lhsT=w_wd[:, t, :].bitcast(E4M3), lhsT_scale=w_sd[:, t, :],
+                    rhs=xt_wg[:, cols].bitcast(E2M1), rhs_scale=xt_sg[:, cols], start=True, stop=True)
+            a_banks.append(bank)
+
+        x4_wg = gather("x4_wg", xt_w, l4, U16)
+        x4_sg = gather("x4_sg", xt_s, l4, U8)
+
+        y_banks = []
+        for h in range(2):
+            cols = slice(h * HALF, (h + 1) * HALF)
+            bank = ps.tile([P, 2, HALF], F32, name=f"y_bank{h}")
+            for g in range(2):
+                rows = slice(g * P, (g + 1) * P)
+                nc.tensor.matmul_mx(
+                    bank[:, g, :],
+                    lhsT=ws_w[:, rows].bitcast(E4M3), lhsT_scale=ws_s[:, rows],
+                    rhs=x4_wg[:, cols].bitcast(E2M1), rhs_scale=x4_sg[:, cols], start=(g == 0), stop=False)
+            y_banks.append(bank)
+
+        out_v = out.rearrange("(g p) j -> p g j", p=P)
+        for h in range(2):
+            cols = slice(h * HALF, (h + 1) * HALF)
+            part = l3[:, h * HALF // 16:(h + 1) * HALF // 16]
+            b_g = tile(f"b_g{h}", [P, PACK, HALF], F32)
+            for t in range(PACK):
+                window = b_sb[:, t * J:(t + 1) * J].indirect(part)
+                if h == 1 and t == 0:
+                    nc.vector.tensor_copy(b_g[:, t, :], window)
+                else:
+                    nc.scalar.activation(b_g[:, t, :], window, COPY)
+            hid = tile(f"hid{h}", [P, HALF * PACK], BF16)
+            nc.vector.tensor_tensor(
+                hid[:].rearrange("p (c i t) -> p c t i", i=4, t=PACK),
+                a_banks[h][:].rearrange("p t (c i) -> p c t i", i=4),
+                b_g[:].rearrange("p t (c i) -> p c t i", i=4),
+                MAX)
+            hq_w = tile(f"hq_w{h}", [P, HALF], U32)
+            hq_s = tile(f"hq_s{h}", [P, HALF], U8)
+            nc.vector.quantize_mx(hq_w[:].bitcast(E5M2), hq_s[:], hid[:])
+            for g in range(2):
+                rows = slice(g * P, (g + 1) * P)
+                nc.tensor.matmul_mx(
+                    y_banks[h][:, g, :],
+                    lhsT=wb_w[:, rows].bitcast(E2M1), lhsT_scale=wb_s[:, rows],
+                    rhs=hq_w[:].bitcast(E5M2), rhs_scale=hq_s[:], start=False, stop=(g == 1))
+            y_sb = tile(f"y_sb{h}", [P, 2, HALF], F32)
+            nc.scalar.copy(y_sb[:], y_banks[h][:])
+            nc.sync.dma_start(out_v[:, :, cols], y_sb[:])

@@ -43,9 +43,14 @@ def tile_list_partner_twotab_further_plain_kernel(
             queue.dma_start(dst[:].bitcast(I32), src.bitcast(I32))
             return dst
 
-        def load_scale_rows(queue, dst, src, q):
-            rows = src[0, 4 * q:4 * q + 4, :].bitcast(I32)
-            queue.dma_start(dst[32 * q:32 * q + 32, :].bitcast(I32), rows.unsqueeze(0).to_broadcast([8, *rows.shape]))
+        def load_scales(queue, dst, src):
+            rows = src[0].bitcast(I32)
+            queue.dma_start(dst.bitcast(I32), rows.unsqueeze(1).to_broadcast([16, 8, rows.shape[1]]))
+
+        def place_rows(queue, plane):
+            words = plane[:].bitcast(I32)
+            for r in range(1, 4):
+                queue.dma_start(words[r:P:32, :], words[8 * r:P:32, :])
 
         def fp8(words):
             return words[0].rearrange("p c t -> p (c t)")
@@ -55,74 +60,76 @@ def tile_list_partner_twotab_further_plain_kernel(
         w2_s = tile("w2_s", [P, R], U8)
         xt_s = tile("xt_s", [P, T], U8)
         w_s = tile("w_s", [P, R], U8)
-        ws_s = tile("ws_s", [P, N], U8)
-        wb_s = tile("wb_s", [P, N], U8)
-        l2 = load_list("l2", offs2)
-        load_scale_rows(sc, xo_s, xo_scales, 0)
-        load_scale_rows(sy, xo_s, xo_scales, 1)
-        load_scale_rows(sc, xo_s, xo_scales, 2)
-        load_scale_rows(sy, xo_s, xo_scales, 3)
-        load_scale_rows(sc, w2_s, w2_scales, 0)
-        xo_w = load_words(sy, "xo_w", fp8(xo_words), Z, U32)
-        load_scale_rows(sc, w2_s, w2_scales, 1)
-        w2_w = load_words(gp, "w2_w", w2_words[0], R, U16)
-        load_scale_rows(gp, w2_s, w2_scales, 2)
-        load_scale_rows(sy, w2_s, w2_scales, 3)
-        w_w = load_words(sy, "w_w", fp8(w_words), R, U32)
-        l1 = load_list("l1", offs)
-        xt_w = load_words(sy, "xt_w", xt_words[0], T, U16)
-        load_scale_rows(sy, xt_s, xt_scales, 0)
-        load_scale_rows(sy, xt_s, xt_scales, 1)
-        load_scale_rows(sy, xt_s, xt_scales, 2)
-        load_scale_rows(sy, xt_s, xt_scales, 3)
-        l3 = load_list("l3", offs3)
-        load_scale_rows(sy, w_s, w_scales, 0)
-        load_scale_rows(sy, w_s, w_scales, 1)
-        load_scale_rows(sy, w_s, w_scales, 2)
-        load_scale_rows(sy, w_s, w_scales, 3)
-        l4 = load_list("l4", offs4)
-        ws_w = load_words(gp, "ws_w", fp8(ws_words), N, U32)
-        wb_w = load_words(gp, "wb_w", wb_words[0], N, U16)
-        load_scale_rows(sy, ws_s, ws_scales, 0)
-        load_scale_rows(sy, ws_s, ws_scales, 1)
-        load_scale_rows(sy, ws_s, ws_scales, 2)
-        load_scale_rows(sy, ws_s, ws_scales, 3)
-        load_scale_rows(gp, wb_s, wb_scales, 0)
-        load_scale_rows(gp, wb_s, wb_scales, 1)
-        load_scale_rows(sy, wb_s, wb_scales, 2)
-        load_scale_rows(sy, wb_s, wb_scales, 3)
+        plane_b = tile("plane_b", [P, R + J], U8)
+        plane_a = tile("plane_a", [P, R + 2 * J + 2 * N], U8)
+        w2_sd, xo_sp = plane_b[:, 0:R], plane_b[:, R:R + J]
+        w_sd, xt_sp, x4_sp = plane_a[:, 0:R], plane_a[:, R:R + J], plane_a[:, R + J:R + 2 * J]
+        ws_s, wb_s = plane_a[:, R + 2 * J:R + 2 * J + N], plane_a[:, R + 2 * J + N:R + 2 * J + 2 * N]
 
-        def gather(name, window, offsets, dtype):
-            dst = tile(name, [P, J], dtype)
-            nc.vector.tensor_copy(dst[:], window[:].indirect(offsets[:]))
-            return dst
+        def gather(dst, window, offsets):
+            nc.vector.tensor_copy(dst, window[:].indirect(offsets[:]))
 
-        def deal(copy, name, src, dtype):
+        def deal_words(copy, name, src, dtype):
             dst = tile(name, [P, PACK, P], dtype)
             copy(dst[:].rearrange("p t m -> p m t"), src[:].rearrange("p (m t) -> p m t", t=PACK))
             return dst
 
-        w2_wd = deal(nc.scalar.copy, "w2_wd", w2_w, U16)
-        w_wd = deal(nc.scalar.copy, "w_wd", w_w, U32)
-        xo_sg = gather("xo_sg", xo_s, l2, U8)
-        xo_wg = gather("xo_wg", xo_w, l2, U32)
-        w2_sd = deal(nc.vector.tensor_copy, "w2_sd", w2_s, U8)
+        def deal_scales(dst, src):
+            nc.gpsimd.tensor_copy(dst.rearrange("p (t m) -> p t m", t=PACK), src[:].rearrange("p (m t) -> p t m", t=PACK))
 
-        b_sb = tile("b_sb", [P, PACK * J], F32)
-        for u in range(2):
-            bank = ps.tile([P, 2 * J], F32, name=f"b_bank{u}")
-            for e in range(2):
-                t = 2 * u + e
-                nc.tensor.matmul_mx(
-                    bank[:, e * J:(e + 1) * J],
-                    lhsT=w2_wd[:, t, :].bitcast(E2M1), lhsT_scale=w2_sd[:, t, :],
-                    rhs=xo_wg[:].bitcast(E4M3), rhs_scale=xo_sg[:], start=True, stop=True)
-            nc.scalar.copy(b_sb[:, 2 * u * J:2 * (u + 1) * J], bank[:])
+        l2 = load_list("l2", offs2)
+        load_scales(sc, xo_s[:], xo_scales)
+        l1 = load_list("l1", offs)
+        load_scales(sc, w2_s[:], w2_scales)
+        l4 = load_list("l4", offs4)
+        load_scales(sc, xt_s[:], xt_scales)
+        load_scales(sc, w_s[:], w_scales)
+        xo_w = load_words(sy, "xo_w", fp8(xo_words), Z, U32)
+        w2_w = load_words(sy, "w2_w", w2_words[0], R, U16)
+        xt_w = load_words(sy, "xt_w", xt_words[0], T, U16)
+        load_scales(sy, ws_s, ws_scales)
+        load_scales(sy, wb_s, wb_scales)
 
-        xt_wg = gather("xt_wg", xt_w, l1, U16)
-        xt_sg = gather("xt_sg", xt_s, l1, U8)
-        w_sd = deal(nc.vector.tensor_copy, "w_sd", w_s, U8)
+        xo_sg = tile("xo_sg", [P, J], U8)
+        gather(xo_sg[:], xo_s, l2)
+        nc.vector.tensor_copy(xo_sp.bitcast(I32), xo_sg[:].bitcast(I32))
+        deal_scales(w2_sd, w2_s)
+        place_rows(sy, plane_b)
+        w_w = load_words(sy, "w_w", fp8(w_words), R, U32)
+        l3 = load_list("l3", offs3)
 
+        xt_sg = tile("xt_sg", [P, 2 * J], U8)
+        gather(xt_sg[:, 0:J], xt_s, l1)
+        gather(xt_sg[:, J:2 * J], xt_s, l4)
+        nc.vector.tensor_copy(plane_a[:, R:R + 2 * J].bitcast(I32), xt_sg[:].bitcast(I32))
+        deal_scales(w_sd, w_s)
+        place_rows(sy, plane_a)
+        ws_w = load_words(sy, "ws_w", fp8(ws_words), N, U32)
+        wb_w = load_words(sy, "wb_w", wb_words[0], N, U16)
+
+        w2_wd = deal_words(nc.scalar.copy, "w2_wd", w2_w, U16)
+        xo_wg = tile("xo_wg", [P, J], U32)
+        gather(xo_wg[:], xo_w, l2)
+        xt_wg = tile("xt_wg", [P, J], U16)
+        gather(xt_wg[:], xt_w, l1)
+        x4_wg = tile("x4_wg", [P, J], U16)
+        gather(x4_wg[:], xt_w, l4)
+
+        b_sb = []
+        for t in range(PACK):
+            bank = ps.tile([P, J], F32, name=f"b_bank{t}", tag=f"bank{t}")
+            nc.tensor.matmul_mx(
+                bank[:],
+                lhsT=w2_wd[:, t, :].bitcast(E2M1), lhsT_scale=w2_sd[:, t * P:(t + 1) * P],
+                rhs=xo_wg[:].bitcast(E4M3), rhs_scale=xo_sp, start=True, stop=True)
+            rows_t = tile(f"b_sb{t}", [P, J], F32)
+            if t % 2 == 0:
+                nc.scalar.copy(rows_t[:], bank[:])
+            else:
+                nc.vector.tensor_copy(rows_t[:], bank[:])
+            b_sb.append(rows_t)
+
+        w_wd = deal_words(nc.vector.tensor_copy, "w_wd", w_w, U32)
         a_banks = []
         for h in range(2):
             cols = slice(h * HALF, (h + 1) * HALF)
@@ -130,33 +137,29 @@ def tile_list_partner_twotab_further_plain_kernel(
             for t in range(PACK):
                 nc.tensor.matmul_mx(
                     bank[:, t, :],
-                    lhsT=w_wd[:, t, :].bitcast(E4M3), lhsT_scale=w_sd[:, t, :],
-                    rhs=xt_wg[:, cols].bitcast(E2M1), rhs_scale=xt_sg[:, cols], start=True, stop=True)
+                    lhsT=w_wd[:, t, :].bitcast(E4M3), lhsT_scale=w_sd[:, t * P:(t + 1) * P],
+                    rhs=xt_wg[:, cols].bitcast(E2M1), rhs_scale=xt_sp[:, cols], start=True, stop=True)
             a_banks.append(bank)
 
-        x4_wg = gather("x4_wg", xt_w, l4, U16)
-        x4_sg = gather("x4_sg", xt_s, l4, U8)
-
-        y_banks = []
+        y_banks = {}
         for h in range(2):
             cols = slice(h * HALF, (h + 1) * HALF)
-            bank = ps.tile([P, 2, HALF], F32, name=f"y_bank{h}")
             for g in range(2):
                 rows = slice(g * P, (g + 1) * P)
+                bank = ps.tile([P, HALF], F32, name=f"y_bank{h}{g}", tag=f"bank{2 * h + g}")
                 nc.tensor.matmul_mx(
-                    bank[:, g, :],
+                    bank[:],
                     lhsT=ws_w[:, rows].bitcast(E4M3), lhsT_scale=ws_s[:, rows],
-                    rhs=x4_wg[:, cols].bitcast(E2M1), rhs_scale=x4_sg[:, cols], start=(g == 0), stop=False)
-            y_banks.append(bank)
+                    rhs=x4_wg[:, cols].bitcast(E2M1), rhs_scale=x4_sp[:, cols], start=True, stop=False)
+                y_banks[h, g] = bank
 
-        out_v = out.rearrange("(g p) j -> p g j", p=P)
         for h in range(2):
             cols = slice(h * HALF, (h + 1) * HALF)
             part = l3[:, h * HALF // 16:(h + 1) * HALF // 16]
             b_g = tile(f"b_g{h}", [P, PACK, HALF], F32)
             for t in range(PACK):
-                window = b_sb[:, t * J:(t + 1) * J].indirect(part)
-                if h == 1 and t == 0:
+                window = b_sb[t][:].indirect(part)
+                if t == 3 or (h == 0 and t == 1):
                     nc.vector.tensor_copy(b_g[:, t, :], window)
                 else:
                     nc.scalar.activation(b_g[:, t, :], window, COPY)
@@ -172,9 +175,14 @@ def tile_list_partner_twotab_further_plain_kernel(
             for g in range(2):
                 rows = slice(g * P, (g + 1) * P)
                 nc.tensor.matmul_mx(
-                    y_banks[h][:, g, :],
+                    y_banks[h, g][:],
                     lhsT=wb_w[:, rows].bitcast(E2M1), lhsT_scale=wb_s[:, rows],
-                    rhs=hq_w[:].bitcast(E5M2), rhs_scale=hq_s[:], start=False, stop=(g == 1))
-            y_sb = tile(f"y_sb{h}", [P, 2, HALF], F32)
-            nc.scalar.copy(y_sb[:], y_banks[h][:])
-            nc.sync.dma_start(out_v[:, :, cols], y_sb[:])
+                    rhs=hq_w[:].bitcast(E5M2), rhs_scale=hq_s[:], start=False, stop=True)
+            for g in range(2):
+                rows = slice(g * P, (g + 1) * P)
+                y_sb = tile(f"y_sb{h}{g}", [P, HALF], F32)
+                if h == 1 and g == 1:
+                    nc.vector.tensor_copy(y_sb[:], y_banks[h, g][:])
+                else:
+                    nc.scalar.copy(y_sb[:], y_banks[h, g][:])
+                nc.sync.dma_start(out[rows, cols], y_sb[:])

@@ -181,8 +181,9 @@ def tile_list_partner_twotab_further_plain_kernel(
             for g in range(2):
                 rows = slice(g * P, (g + 1) * P)
                 y_sb = tile(f"y_sb{h}{g}", [P, HALF], F32)
-                if h == 1 and g == 1:
-                    nc.vector.tensor_copy(y_sb[:], y_banks[h, g][:])
-                else:
+                if g == 0:
                     nc.scalar.copy(y_sb[:], y_banks[h, g][:])
-                nc.sync.dma_start(out[rows, cols], y_sb[:])
+                    nc.scalar.dma_start(out[rows, cols], y_sb[:])
+                else:
+                    nc.vector.tensor_copy(y_sb[:], y_banks[h, g][:])
+                    nc.sync.dma_start(out[rows, cols], y_sb[:])

from contextlib import ExitStack

import concourse.mybir as mybir

F32 = mybir.dt.float32
BF16 = mybir.dt.bfloat16
I32 = mybir.dt.int32
U32 = mybir.dt.uint32
U16 = mybir.dt.uint16
U8 = mybir.dt.uint8
E4M3 = mybir.dt.float8_e4m3fn_x4
E5M2 = mybir.dt.float8_e5m2_x4
E2M1 = mybir.dt.float4_e2m1fn_x4
COPY = mybir.ActivationFunctionType.Copy
MAX = mybir.AluOpType.max

P = 128
PACK = 4
T, Z, J, R, N = 1024, 1024, 256, 512, 256
HALF = J // 2
FLOPS = 2 * 512 * J * (R + R + N + N)


def tile_list_partner_twotab_further_plain_kernel(
    tc, xt_words, xt_scales, w_words, w_scales, xo_words, xo_scales, w2_words, w2_scales,
    wb_words, wb_scales, ws_words, ws_scales, offs, offs2, offs3, offs4, out,
):
    nc = tc.nc
    with ExitStack() as ctx:
        sb = ctx.enter_context(tc.tile_pool(name="sb", bufs=1))
        ps = ctx.enter_context(tc.psum_pool(name="ps", bufs=1))

        def tile(name, shape, dtype):
            return sb.tile(shape, dtype, name=name, align_bytes=64)

        def load_list(name, src):
            dst = tile(name, [P, J // 16], U16)
            nc.sync.dma_start(dst[:], src)
            return dst

        def load_words(queue, name, src, cols, dtype):
            dst = tile(name, [P, cols], dtype)
            queue.dma_start(dst[:].bitcast(I32), src.bitcast(I32))
            return dst

        def load_scales(queue, dst, src):
            rows = src[0].bitcast(I32)
            queue.dma_start(dst.bitcast(I32), rows.unsqueeze(1).to_broadcast([16, 8, rows.shape[1]]))

        def place_rows(queue, plane):
            words = plane[:].bitcast(I32)
            for r in range(1, 4):
                queue.dma_start(words[r:P:32, :], words[8 * r:P:32, :])

        def fp8(words):
            return words[0].rearrange("p c t -> p (c t)")

        sy, sc, gp = nc.sync, nc.scalar, nc.gpsimd
        xo_s = tile("xo_s", [P, Z], U8)
        w2_s = tile("w2_s", [P, R], U8)
        xt_s = tile("xt_s", [P, T], U8)
        w_s = tile("w_s", [P, R], U8)
        plane_b = tile("plane_b", [P, R + J], U8)
        plane_a = tile("plane_a", [P, R + 2 * J + 2 * N], U8)
        w2_sd, xo_sp = plane_b[:, 0:R], plane_b[:, R:R + J]
        w_sd, xt_sp, x4_sp = plane_a[:, 0:R], plane_a[:, R:R + J], plane_a[:, R + J:R + 2 * J]
        ws_s, wb_s = plane_a[:, R + 2 * J:R + 2 * J + N], plane_a[:, R + 2 * J + N:R + 2 * J + 2 * N]

        def gather(dst, window, offsets):
            nc.vector.tensor_copy(dst, window[:].indirect(offsets[:]))

        def deal_words(copy, name, src, dtype):
            dst = tile(name, [P, PACK, P], dtype)
            copy(dst[:].rearrange("p t m -> p m t"), src[:].rearrange("p (m t) -> p m t", t=PACK))
            return dst

        def deal_scales(dst, src):
            nc.gpsimd.tensor_copy(dst.rearrange("p (t m) -> p t m", t=PACK), src[:].rearrange("p (m t) -> p t m", t=PACK))

        l2 = load_list("l2", offs2)
        load_scales(sc, xo_s[:], xo_scales)
        l1 = load_list("l1", offs)
        load_scales(sc, w2_s[:], w2_scales)
        l4 = load_list("l4", offs4)
        load_scales(sc, xt_s[:], xt_scales)
        load_scales(sc, w_s[:], w_scales)
        xo_w = load_words(sy, "xo_w", fp8(xo_words), Z, U32)
        w2_w = load_words(sy, "w2_w", w2_words[0], R, U16)
        xt_w = load_words(sy, "xt_w", xt_words[0], T, U16)
        load_scales(sy, ws_s, ws_scales)
        load_scales(sy, wb_s, wb_scales)

        xo_sg = tile("xo_sg", [P, J], U8)
        gather(xo_sg[:], xo_s, l2)
        nc.vector.tensor_copy(xo_sp.bitcast(I32), xo_sg[:].bitcast(I32))
        deal_scales(w2_sd, w2_s)
        place_rows(sy, plane_b)
        w_w = load_words(sy, "w_w", fp8(w_words), R, U32)
        l3 = load_list("l3", offs3)

        xt_sg = tile("xt_sg", [P, 2 * J], U8)
        gather(xt_sg[:, 0:J], xt_s, l1)
        gather(xt_sg[:, J:2 * J], xt_s, l4)
        nc.vector.tensor_copy(plane_a[:, R:R + 2 * J].bitcast(I32), xt_sg[:].bitcast(I32))
        deal_scales(w_sd, w_s)
        place_rows(sy, plane_a)
        ws_w = load_words(sy, "ws_w", fp8(ws_words), N, U32)
        wb_w = load_words(sy, "wb_w", wb_words[0], N, U16)

        w2_wd = deal_words(nc.scalar.copy, "w2_wd", w2_w, U16)
        xo_wg = tile("xo_wg", [P, J], U32)
        gather(xo_wg[:], xo_w, l2)
        xt_wg = tile("xt_wg", [P, J], U16)
        gather(xt_wg[:], xt_w, l1)
        x4_wg = tile("x4_wg", [P, J], U16)
        gather(x4_wg[:], xt_w, l4)

        b_sb = []
        for t in range(PACK):
            bank = ps.tile([P, J], F32, name=f"b_bank{t}", tag=f"bank{t}")
            nc.tensor.matmul_mx(
                bank[:],
                lhsT=w2_wd[:, t, :].bitcast(E2M1), lhsT_scale=w2_sd[:, t * P:(t + 1) * P],
                rhs=xo_wg[:].bitcast(E4M3), rhs_scale=xo_sp, start=True, stop=True)
            rows_t = tile(f"b_sb{t}", [P, J], F32)
            if t % 2 == 0:
                nc.scalar.copy(rows_t[:], bank[:])
            else:
                nc.vector.tensor_copy(rows_t[:], bank[:])
            b_sb.append(rows_t)

        w_wd = deal_words(nc.vector.tensor_copy, "w_wd", w_w, U32)
        a_banks = []
        for h in range(2):
            cols = slice(h * HALF, (h + 1) * HALF)
            bank = ps.tile([P, PACK, HALF], F32, name=f"a_bank{h}")
            for t in range(PACK):
                nc.tensor.matmul_mx(
                    bank[:, t, :],
                    lhsT=w_wd[:, t, :].bitcast(E4M3), lhsT_scale=w_sd[:, t * P:(t + 1) * P],
                    rhs=xt_wg[:, cols].bitcast(E2M1), rhs_scale=xt_sp[:, cols], start=True, stop=True)
            a_banks.append(bank)

        y_banks = {}
        for h in range(2):
            cols = slice(h * HALF, (h + 1) * HALF)
            for g in range(2):
                rows = slice(g * P, (g + 1) * P)
                bank = ps.tile([P, HALF], F32, name=f"y_bank{h}{g}", tag=f"bank{2 * h + g}")
                nc.tensor.matmul_mx(
                    bank[:],
                    lhsT=ws_w[:, rows].bitcast(E4M3), lhsT_scale=ws_s[:, rows],
                    rhs=x4_wg[:, cols].bitcast(E2M1), rhs_scale=x4_sp[:, cols], start=True, stop=False)
                y_banks[h, g] = bank

        for h in range(2):
            cols = slice(h * HALF, (h + 1) * HALF)
            part = l3[:, h * HALF // 16:(h + 1) * HALF // 16]
            b_g = tile(f"b_g{h}", [P, PACK, HALF], F32)
            for t in range(PACK):
                window = b_sb[t][:].indirect(part)
                if t == 3 or (h == 0 and t == 1):
                    nc.vector.tensor_copy(b_g[:, t, :], window)
                else:
                    nc.scalar.activation(b_g[:, t, :], window, COPY)
            hid = tile(f"hid{h}", [P, HALF * PACK], BF16)
            nc.vector.tensor_tensor(
                hid[:].rearrange("p (c i t) -> p c t i", i=4, t=PACK),
                a_banks[h][:].rearrange("p t (c i) -> p c t i", i=4),
                b_g[:].rearrange("p t (c i) -> p c t i", i=4),
                MAX)
            hq_w = tile(f"hq_w{h}", [P, HALF], U32)
            hq_s = tile(f"hq_s{h}", [P, HALF], U8)
            nc.vector.quantize_mx(hq_w[:].bitcast(E5M2), hq_s[:], hid[:])
            for g in range(2):
                rows = slice(g * P, (g + 1) * P)
                nc.tensor.matmul_mx(
                    y_banks[h, g][:],
                    lhsT=wb_w[:, rows].bitcast(E2M1), lhsT_scale=wb_s[:, rows],
                    rhs=hq_w[:].bitcast(E5M2), rhs_scale=hq_s[:], start=False, stop=True)
            for g in range(2):
                rows = slice(g * P, (g + 1) * P)
                y_sb = tile(f"y_sb{h}{g}", [P, HALF], F32)
                if g == 0:
                    nc.scalar.copy(y_sb[:], y_banks[h, g][:])
                    nc.scalar.dma_start(out[rows, cols], y_sb[:])
                else:
                    nc.vector.tensor_copy(y_sb[:], y_banks[h, g][:])
                    nc.sync.dma_start(out[rows, cols], y_sb[:])
